import numpy as np
import ml_dtypes


def mxq(x, axis, fmt="e4m3"):
    dtype, down = {"e4m3": (ml_dtypes.float8_e4m3fn, 7), "e5m2": (ml_dtypes.float8_e5m2, 14)}[fmt]
    v = np.moveaxis(np.asarray(x, np.float32).astype(ml_dtypes.bfloat16).astype(np.float64), axis, -1)
    blocks = v.reshape(v.shape[:-1] + (-1, 32))
    amax = np.abs(blocks).max(-1, keepdims=True)
    byte = np.maximum(np.where(amax > 0, np.frexp(amax)[1] - 1 + 127, 0) - down, 1)
    scale = np.exp2(byte - 127.0)
    codes = (blocks / scale).astype(np.float32).astype(dtype).astype(np.float64)
    return np.moveaxis((codes * scale).reshape(v.shape), -1, axis)


WIDE = False


def mx_kscale(k):
    if not WIDE:
        return np.ones(k)
    levels = np.array([10, -10, 5, -5, 0])
    if k % 512:
        return np.exp2(np.random.permutation(np.resize(levels, k // 32))).repeat(32)
    a = np.empty((k // 512, 16))
    for p in range(k // 512):
        a[p, :8] = np.random.permutation(np.resize(levels, 8))
        for g in range(8):
            far = levels[np.abs(levels - a[p, g]) >= 10]
            a[p, g + 8] = far[np.random.randint(len(far))]
    return np.exp2(a.ravel()).repeat(32)


def f64(x):
    return np.asarray(x).astype(np.float64)


def striped8(idx):
    return np.asarray(idx).reshape(8, -1, 16).transpose(0, 2, 1).reshape(128, -1).astype(np.uint16)


def unstriped8(offs):
    return offs.reshape(8, 16, -1).transpose(0, 2, 1).reshape(8, -1).astype(np.int64)


def pick8(x, idx, run):
    r = np.arange(len(x))
    return x[r[:, None], idx[r % (8 * run) // run]]


E2M1 = np.array([0.0, 0.5, 1.0, 1.5, 2.0, 3.0, 4.0, 6.0, -0.0, -0.5, -1.0, -1.5, -2.0, -3.0, -4.0, -6.0])


def pack_weight(w, fmt):
    k, n = w.shape
    w = f64(np.asarray(w, np.float32).astype(ml_dtypes.bfloat16)).reshape(k // 32, 32, n)
    amax = np.abs(w).max(1)
    if fmt == "e4m3":
        byte = np.frexp(amax)[1] - 1 + 127 - 7
    else:
        mant, ex = np.frexp(amax / 6.0)
        byte = np.where(mant > 0.5, ex, ex - 1) + 127
    byte = np.clip(np.where(amax > 0, byte, 1), 1, 254)
    scaled = (w * np.exp2(127.0 - byte)[:, None, :]).reshape(k, n).astype(np.float32)
    by_word = np.ascontiguousarray(scaled.reshape(k // 512, 128, 4, n).transpose(0, 1, 3, 2))
    if fmt == "e4m3":
        words = by_word.astype(ml_dtypes.float8_e4m3fn).view(np.uint8)
    else:
        c = by_word.astype(ml_dtypes.float4_e2m1fn).view(np.uint8) & 0xF
        words = (c[..., 0::2] | (c[..., 1::2] << 4)).reshape(k // 512, 128, 2 * n)
    return np.ascontiguousarray(words), np.ascontiguousarray(byte.astype(np.uint8).reshape(k // 512, 16, n))


def unpack_weight(words, scales, fmt):
    g, _, n = scales.shape
    words = np.ascontiguousarray(words).reshape(g, 128, n, -1)
    if fmt == "e4m3":
        vals = words.view(ml_dtypes.float8_e4m3fn).astype(np.float64)
    else:
        nib = np.empty((g, 128, n, 4), np.uint8)
        nib[..., 0::2] = words & 0xF
        nib[..., 1::2] = words >> 4
        vals = E2M1[nib]
    vals = vals * np.repeat(np.exp2(scales.astype(np.float64) - 127.0), 8, axis=1)[..., None]
    return vals.transpose(0, 1, 3, 2).reshape(g * 512, n)


def sigmoid(v):
    return 1.0 / (1.0 + np.exp(-v))


D, T, U, I, Q = 512, 1024, 1024, 512, 128


def setup_inputs():
    n = np.random.standard_normal
    idx = np.stack([np.random.permutation(T)[:I] for _ in range(8)])
    idx2 = np.stack([np.random.permutation(U)[:I] for _ in range(8)])
    idx3 = np.stack([np.random.permutation(U)[:I] for _ in range(8)])
    fd = mx_kscale(D)
    keysp = pack_weight(n((D, T)) / fd[:, None], "e4m3")
    notesp = pack_weight(n((D, U)) / fd[:, None], "e2m1")
    return {
        "query": (n((D, Q)) * 1.0 / np.sqrt(D) * fd[:, None]).astype(np.float32),
        "keys_words": keysp[0],
        "keys_scales": keysp[1],
        "notes_words": notesp[0],
        "notes_scales": notesp[1],
        "thr": (np.random.uniform(-0.6, 0.6, (Q, 1))).astype(np.float32),
        "slope": (np.random.uniform(1.0, 3.0, (Q, 1))).astype(np.float32),
        "offs": striped8(idx),
        "offs2": striped8(idx2),
        "offs3": striped8(idx3),
    }


def reference(query, keys_words, keys_scales, notes_words, notes_scales, thr, slope, offs, offs2, offs3):
    idx = unstriped8(offs)
    idx2 = unstriped8(offs2)
    idx3 = unstriped8(offs3)
    keysu = unpack_weight(keys_words, keys_scales, "e4m3")
    notesu = unpack_weight(notes_words, notes_scales, "e2m1")
    queryq = mxq(f64(query), 0, "e4m3")
    a = queryq.T @ keysu
    b = queryq.T @ notesu
    s1 = sigmoid(pick8(a, idx, 16) * f64(slope) + f64(thr))
    f1 = np.zeros((Q, U))
    f1[np.arange(Q)[:, None], idx2[np.arange(Q) % 128 // 16]] = s1
    cc = b + f1 * 2.0
    tc2 = np.max(cc, axis=1, keepdims=True)
    y = np.exp(pick8(cc, idx3, 16) - tc2)
    return y

@@ -1,0 +1,124 @@
+from contextlib import ExitStack
+
+import concourse.mybir as mybir
+
+D, T, U, I, Q = 512, 1024, 1024, 512, 128
+FLOPS = 2 * D * Q * (T + U)
+
+F32 = mybir.dt.float32
+BF16 = mybir.dt.bfloat16
+I32 = mybir.dt.int32
+U32 = mybir.dt.uint32
+U16 = mybir.dt.uint16
+U8 = mybir.dt.uint8
+FP8X4 = mybir.dt.float8_e4m3fn_x4
+FP4X4 = mybir.dt.float4_e2m1fn_x4
+ALU = mybir.AluOpType
+ACT = mybir.ActivationFunctionType
+
+P = 128
+PACK = 4
+BANK = 512
+PIECE = 256
+CHUNK = 256
+LIST_COLS = PIECE // 16
+
+
+def load_scale_rows(queue, plane, scales):
+    for quad in range(4):
+        queue.dma_start(
+            out=plane[32 * quad : 32 * quad + 4, :].bitcast(I32),
+            in_=scales[0, 4 * quad : 4 * quad + 4, :].bitcast(I32),
+        )
+
+
+def tile_attend_openedfirst_two_kernel(
+    tc, query, keys_words, keys_scales, notes_words, notes_scales, thr, slope, offs, offs2, offs3, out
+):
+    nc = tc.nc
+    with ExitStack() as ctx:
+        sb = ctx.enter_context(tc.tile_pool(name="sb", bufs=1))
+        ps = ctx.enter_context(tc.psum_pool(name="ps", bufs=1))
+
+        key_plane = sb.tile([P, T], U8, align_bytes=64)
+        note_plane = sb.tile([P, U], U8, align_bytes=64)
+        gates = sb.tile([P, U], F32)
+        nc.vector.memset(key_plane[:].bitcast(I32), 0)
+        nc.vector.memset(note_plane[:].bitcast(I32), 0)
+        nc.vector.memset(gates[:], 0.0)
+
+        q_raw = sb.tile([P, PACK, Q], F32)
+        nc.sync.dma_start(out=q_raw[:], in_=query.rearrange("(p j) q -> p j q", j=PACK))
+        load_scale_rows(nc.scalar, key_plane, keys_scales)
+        key_src = keys_words[0].rearrange("p n t -> p (n t)").bitcast(I32)
+        key_words = []
+        for h in range(T // BANK):
+            words = sb.tile([P, BANK], U32, align_bytes=64, name="key_words%d" % h)
+            nc.sync.dma_start(out=words[:].bitcast(I32), in_=key_src[:, h * BANK : (h + 1) * BANK])
+            key_words.append(words)
+        token_list = sb.tile([P, I // 16], U16)
+        nc.sync.dma_start(token_list[:], offs)
+        thr_col = sb.tile([P, 1], F32)
+        slope_col = sb.tile([P, 1], F32)
+        nc.sync.dma_start(out=slope_col[:], in_=slope)
+        nc.sync.dma_start(out=thr_col[:], in_=thr)
+        gate_list = sb.tile([P, I // 16], U16)
+        nc.sync.dma_start(gate_list[:], offs2)
+        note_words = sb.tile([P, 2 * U], U8, align_bytes=64)
+        nc.sync.dma_start(out=note_words[:].bitcast(I32), in_=notes_words[0].bitcast(I32))
+        load_scale_rows(nc.sync, note_plane, notes_scales)
+        out_list = sb.tile([P, I // 16], U16)
+        nc.sync.dma_start(out_list[:], offs3)
+
+        q_grouped = sb.tile([P, Q, PACK], BF16, align_bytes=64)
+        nc.vector.tensor_copy(out=q_grouped[:], in_=q_raw[:].rearrange("p j q -> p q j"))
+        q_words = sb.tile([P, Q], U32, align_bytes=64)
+        q_plane = sb.tile([P, Q], U8, align_bytes=64)
+        nc.vector.quantize_mx(
+            out=q_words[:].bitcast(FP8X4), scales=q_plane[:], in_=q_grouped[:].rearrange("p q j -> p (q j)")
+        )
+
+        token_scores = sb.tile([P, T], F32)
+        for c in range(T // CHUNK):
+            cols = slice(c * CHUNK, (c + 1) * CHUNK)
+            h, lo = divmod(c * CHUNK, BANK)
+            acc = ps.tile([P, CHUNK], F32, name="token_acc%d" % c)
+            nc.tensor.matmul_mx(
+                out=acc[:], lhsT=q_words[:].bitcast(FP8X4), lhsT_scale=q_plane[:],
+                rhs=key_words[h][:, lo : lo + CHUNK].bitcast(FP8X4), rhs_scale=key_plane[:, cols], start=True, stop=True,
+            )
+            nc.vector.tensor_copy(out=token_scores[:, cols], in_=acc[:])
+
+        note_acc = []
+        for h in range(U // BANK):
+            acc = ps.tile([P, BANK], F32, name="note_acc%d" % h)
+            nc.tensor.matmul_mx(
+                out=acc[:], lhsT=q_words[:].bitcast(FP8X4), lhsT_scale=q_plane[:],
+                rhs=note_words[:, 2 * h * BANK : 2 * (h + 1) * BANK].bitcast(FP4X4),
+                rhs_scale=note_plane[:, h * BANK : (h + 1) * BANK], start=True, stop=True,
+            )
+            note_acc.append(acc)
+
+        for s in range(I // PIECE):
+            entries = slice(s * LIST_COLS, (s + 1) * LIST_COLS)
+            opened = sb.tile([P, PIECE], F32, name="opened%d" % s)
+            nc.scalar.activation(
+                opened[:], token_scores[:].indirect(token_list[:, entries]), ACT.Sigmoid,
+                bias=thr_col[:], scale=slope_col[:],
+            )
+            nc.vector.tensor_copy(gates[:].indirect(gate_list[:, entries]), opened[:])
+
+        sums = sb.tile([P, U], F32)
+        for h in range(U // BANK):
+            cols = slice(h * BANK, (h + 1) * BANK)
+            nc.vector.scalar_tensor_tensor(
+                out=sums[:, cols], in0=gates[:, cols], scalar=2.0, in1=note_acc[h][:], op0=ALU.mult, op1=ALU.add
+            )
+        neg_top = sb.tile([P, 1], F32)
+        nc.vector.tensor_reduce(out=neg_top[:], in_=sums[:], axis=mybir.AxisListType.X, op=ALU.max, negate=True)
+
+        for s in range(I // PIECE):
+            entries = slice(s * LIST_COLS, (s + 1) * LIST_COLS)
+            result = sb.tile([P, PIECE], F32, name="result%d" % s)
+            nc.scalar.activation(result[:], sums[:].indirect(out_list[:, entries]), ACT.Exp, bias=neg_top[:])
+            nc.sync.dma_start(out=out[:, s * PIECE : (s + 1) * PIECE], in_=result[:])

@@ -20,7 +20,7 @@ P = 128
 PACK = 4
 BANK = 512
 PIECE = 256
-CHUNK = 256
+TOKEN_PASSES = (128, 256, 256, 256, 128)
 LIST_COLS = PIECE // 16
 
 
@@ -43,24 +43,20 @@ def tile_attend_openedfirst_two_kernel(
         key_plane = sb.tile([P, T], U8, align_bytes=64)
         note_plane = sb.tile([P, U], U8, align_bytes=64)
         gates = sb.tile([P, U], F32)
-        nc.vector.memset(key_plane[:].bitcast(I32), 0)
-        nc.vector.memset(note_plane[:].bitcast(I32), 0)
         nc.vector.memset(gates[:], 0.0)
 
         q_raw = sb.tile([P, PACK, Q], F32)
         nc.sync.dma_start(out=q_raw[:], in_=query.rearrange("(p j) q -> p j q", j=PACK))
         load_scale_rows(nc.scalar, key_plane, keys_scales)
-        key_src = keys_words[0].rearrange("p n t -> p (n t)").bitcast(I32)
-        key_words = []
-        for h in range(T // BANK):
-            words = sb.tile([P, BANK], U32, align_bytes=64, name="key_words%d" % h)
-            nc.sync.dma_start(out=words[:].bitcast(I32), in_=key_src[:, h * BANK : (h + 1) * BANK])
-            key_words.append(words)
+        key_words = sb.tile([P, T], U32, align_bytes=64)
+        nc.sync.dma_start(
+            out=key_words[:].bitcast(I32), in_=keys_words[0].rearrange("p n t -> p (n t)").bitcast(I32)
+        )
         token_list = sb.tile([P, I // 16], U16)
         nc.sync.dma_start(token_list[:], offs)
         thr_col = sb.tile([P, 1], F32)
         slope_col = sb.tile([P, 1], F32)
-        nc.sync.dma_start(out=slope_col[:], in_=slope)
+        nc.gpsimd.dma_start(out=slope_col[:], in_=slope)
         nc.sync.dma_start(out=thr_col[:], in_=thr)
         gate_list = sb.tile([P, I // 16], U16)
         nc.sync.dma_start(gate_list[:], offs2)
@@ -71,7 +67,9 @@ def tile_attend_openedfirst_two_kernel(
         nc.sync.dma_start(out_list[:], offs3)
 
         q_grouped = sb.tile([P, Q, PACK], BF16, align_bytes=64)
-        nc.vector.tensor_copy(out=q_grouped[:], in_=q_raw[:].rearrange("p j q -> p q j"))
+        nc.vector.tensor_copy(
+            out=q_grouped[:].rearrange("p (c i) j -> p c j i", i=4), in_=q_raw[:].rearrange("p j (c i) -> p c j i", i=4)
+        )
         q_words = sb.tile([P, Q], U32, align_bytes=64)
         q_plane = sb.tile([P, Q], U8, align_bytes=64)
         nc.vector.quantize_mx(
@@ -79,15 +77,16 @@ def tile_attend_openedfirst_two_kernel(
         )
 
         token_scores = sb.tile([P, T], F32)
-        for c in range(T // CHUNK):
-            cols = slice(c * CHUNK, (c + 1) * CHUNK)
-            h, lo = divmod(c * CHUNK, BANK)
-            acc = ps.tile([P, CHUNK], F32, name="token_acc%d" % c)
+        start = 0
+        for c, width in enumerate(TOKEN_PASSES):
+            cols = slice(start, start + width)
+            acc = ps.tile([P, width], F32, name="token_acc%d" % c)
             nc.tensor.matmul_mx(
                 out=acc[:], lhsT=q_words[:].bitcast(FP8X4), lhsT_scale=q_plane[:],
-                rhs=key_words[h][:, lo : lo + CHUNK].bitcast(FP8X4), rhs_scale=key_plane[:, cols], start=True, stop=True,
+                rhs=key_words[:, cols].bitcast(FP8X4), rhs_scale=key_plane[:, cols], start=True, stop=True,
             )
             nc.vector.tensor_copy(out=token_scores[:, cols], in_=acc[:])
+            start = start + width
 
         note_acc = []
         for h in range(U // BANK):

@@ -19,9 +19,10 @@ ACT = mybir.ActivationFunctionType
 P = 128
 PACK = 4
 BANK = 512
+TOKEN_PASS = 256
 PIECE = 256
-TOKEN_PASSES = (128, 256, 256, 256, 128)
 LIST_COLS = PIECE // 16
+BLOCK_WORDS = 8
 
 
 def load_scale_rows(queue, plane, scales):
@@ -40,53 +41,62 @@ def tile_attend_openedfirst_two_kernel(
         sb = ctx.enter_context(tc.tile_pool(name="sb", bufs=1))
         ps = ctx.enter_context(tc.psum_pool(name="ps", bufs=1))
 
-        key_plane = sb.tile([P, T], U8, align_bytes=64)
-        note_plane = sb.tile([P, U], U8, align_bytes=64)
         gates = sb.tile([P, U], F32)
         nc.vector.memset(gates[:], 0.0)
 
         q_raw = sb.tile([P, PACK, Q], F32)
         nc.sync.dma_start(out=q_raw[:], in_=query.rearrange("(p j) q -> p j q", j=PACK))
+        key_plane = sb.tile([P, T], U8, align_bytes=64)
         load_scale_rows(nc.scalar, key_plane, keys_scales)
-        key_words = sb.tile([P, T], U32, align_bytes=64)
-        nc.sync.dma_start(
-            out=key_words[:].bitcast(I32), in_=keys_words[0].rearrange("p n t -> p (n t)").bitcast(I32)
-        )
         token_list = sb.tile([P, I // 16], U16)
         nc.sync.dma_start(token_list[:], offs)
-        thr_col = sb.tile([P, 1], F32)
-        slope_col = sb.tile([P, 1], F32)
-        nc.gpsimd.dma_start(out=slope_col[:], in_=slope)
-        nc.sync.dma_start(out=thr_col[:], in_=thr)
+        key_src = keys_words[0].rearrange("p n t -> p (n t)").bitcast(I32)
+        key_words = []
+        for h in range(T // BANK):
+            words = sb.tile([P, BANK], U32, align_bytes=64, name="key_words%d" % h)
+            nc.sync.dma_start(out=words[:].bitcast(I32), in_=key_src[:, h * BANK : (h + 1) * BANK])
+            key_words.append(words)
+        gate_loaded = sb.tile([P, 2, BLOCK_WORDS], F32)
+        nc.scalar.dma_start(out=gate_loaded[:, 0, 0:1], in_=slope)
+        nc.scalar.dma_start(out=gate_loaded[:, 1, 0:1], in_=thr)
         gate_list = sb.tile([P, I // 16], U16)
         nc.sync.dma_start(gate_list[:], offs2)
         note_words = sb.tile([P, 2 * U], U8, align_bytes=64)
         nc.sync.dma_start(out=note_words[:].bitcast(I32), in_=notes_words[0].bitcast(I32))
+        note_plane = sb.tile([P, U], U8, align_bytes=64)
         load_scale_rows(nc.sync, note_plane, notes_scales)
         out_list = sb.tile([P, I // 16], U16)
         nc.sync.dma_start(out_list[:], offs3)
 
         q_grouped = sb.tile([P, Q, PACK], BF16, align_bytes=64)
-        nc.vector.tensor_copy(
-            out=q_grouped[:].rearrange("p (c i) j -> p c j i", i=4), in_=q_raw[:].rearrange("p j (c i) -> p c j i", i=4)
-        )
         q_words = sb.tile([P, Q], U32, align_bytes=64)
         q_plane = sb.tile([P, Q], U8, align_bytes=64)
-        nc.vector.quantize_mx(
-            out=q_words[:].bitcast(FP8X4), scales=q_plane[:], in_=q_grouped[:].rearrange("p q j -> p (q j)")
-        )
+        halves = [slice(h * Q // 2, (h + 1) * Q // 2) for h in range(2)]
+        for rows in halves:
+            nc.vector.tensor_copy(
+                out=q_grouped[:, rows, :].rearrange("p (c i) j -> p c j i", i=4),
+                in_=q_raw[:, :, rows].rearrange("p j (c i) -> p c j i", i=4),
+            )
+        for rows in halves:
+            nc.vector.quantize_mx(
+                out=q_words[:, rows].bitcast(FP8X4), scales=q_plane[:, rows],
+                in_=q_grouped[:, rows, :].rearrange("p q j -> p (q j)"),
+            )
 
         token_scores = sb.tile([P, T], F32)
-        start = 0
-        for c, width in enumerate(TOKEN_PASSES):
-            cols = slice(start, start + width)
-            acc = ps.tile([P, width], F32, name="token_acc%d" % c)
+        for start in range(0, T, TOKEN_PASS):
+            cols = slice(start, start + TOKEN_PASS)
+            h, lo = divmod(start, BANK)
+            acc = ps.tile([P, BANK], F32, name="token_acc%d" % start)[:, :TOKEN_PASS]
             nc.tensor.matmul_mx(
-                out=acc[:], lhsT=q_words[:].bitcast(FP8X4), lhsT_scale=q_plane[:],
-                rhs=key_words[:, cols].bitcast(FP8X4), rhs_scale=key_plane[:, cols], start=True, stop=True,
+                out=acc, lhsT=q_words[:].bitcast(FP8X4), lhsT_scale=q_plane[:],
+                rhs=key_words[h][:, lo : lo + TOKEN_PASS].bitcast(FP8X4), rhs_scale=key_plane[:, cols],
+                start=True, stop=True,
             )
-            nc.vector.tensor_copy(out=token_scores[:, cols], in_=acc[:])
-            start = start + width
+            nc.vector.tensor_copy(out=token_scores[:, cols], in_=acc)
+
+        gate_terms = sb.tile([P, 2], F32)
+        nc.vector.tensor_copy(out=gate_terms[:], in_=gate_loaded[:, :, 0])
 
         note_acc = []
         for h in range(U // BANK):
@@ -103,7 +113,7 @@ def tile_attend_openedfirst_two_kernel(
             opened = sb.tile([P, PIECE], F32, name="opened%d" % s)
             nc.scalar.activation(
                 opened[:], token_scores[:].indirect(token_list[:, entries]), ACT.Sigmoid,
-                bias=thr_col[:], scale=slope_col[:],
+                bias=gate_terms[:, 1:2], scale=gate_terms[:, 0:1],
             )
             nc.vector.tensor_copy(gates[:].indirect(gate_list[:, entries]), opened[:])
 

@@ -18,19 +18,29 @@ ACT = mybir.ActivationFunctionType
 
 P = 128
 PACK = 4
+QUADRANT = 32
+SCALE_ROWS = 4
+HEAD_ROWS = 16
+MX_ALIGN = 64
 BANK = 512
+LINE = 4
+DMA_BLOCK = 8
 TOKEN_PASS = 256
 PIECE = 256
-LIST_COLS = PIECE // 16
-BLOCK_WORDS = 8
+SPLIT = 704
 
 
-def load_scale_rows(queue, plane, scales):
-    for quad in range(4):
+def load_scale_rows(queues, plane, scales):
+    for quad, queue in enumerate(queues):
         queue.dma_start(
-            out=plane[32 * quad : 32 * quad + 4, :].bitcast(I32),
-            in_=scales[0, 4 * quad : 4 * quad + 4, :].bitcast(I32),
+            out=plane[QUADRANT * quad : QUADRANT * quad + SCALE_ROWS, :].bitcast(I32),
+            in_=scales[0, SCALE_ROWS * quad : SCALE_ROWS * (quad + 1), :].bitcast(I32),
         )
+
+
+def list_piece(list_tile, piece):
+    width = PIECE // HEAD_ROWS
+    return list_tile[:, piece * width : (piece + 1) * width]
 
 
 def tile_attend_openedfirst_two_kernel(
@@ -45,89 +55,99 @@ def tile_attend_openedfirst_two_kernel(
         nc.vector.memset(gates[:], 0.0)
 
         q_raw = sb.tile([P, PACK, Q], F32)
-        nc.sync.dma_start(out=q_raw[:], in_=query.rearrange("(p j) q -> p j q", j=PACK))
-        key_plane = sb.tile([P, T], U8, align_bytes=64)
-        load_scale_rows(nc.scalar, key_plane, keys_scales)
-        token_list = sb.tile([P, I // 16], U16)
+        nc.sync.dma_start(out=q_raw[:], in_=query.rearrange("(p r) q -> p r q", r=PACK))
+        key_plane = sb.tile([P, T], U8, align_bytes=MX_ALIGN)
+        load_scale_rows((nc.sync, nc.sync, nc.scalar, nc.scalar), key_plane, keys_scales)
+        token_list = sb.tile([P, I // HEAD_ROWS], U16)
         nc.sync.dma_start(token_list[:], offs)
-        key_src = keys_words[0].rearrange("p n t -> p (n t)").bitcast(I32)
+        key_src = keys_words[0].rearrange("p t r -> p (t r)").bitcast(I32)
         key_words = []
-        for h in range(T // BANK):
-            words = sb.tile([P, BANK], U32, align_bytes=64, name="key_words%d" % h)
-            nc.sync.dma_start(out=words[:].bitcast(I32), in_=key_src[:, h * BANK : (h + 1) * BANK])
+        for half in range(T // BANK):
+            words = sb.tile([P, BANK], U32, align_bytes=MX_ALIGN, name="key_words%d" % half)
+            nc.sync.dma_start(out=words[:].bitcast(I32), in_=key_src[:, half * BANK : (half + 1) * BANK])
             key_words.append(words)
-        gate_loaded = sb.tile([P, 2, BLOCK_WORDS], F32)
-        nc.scalar.dma_start(out=gate_loaded[:, 0, 0:1], in_=slope)
-        nc.scalar.dma_start(out=gate_loaded[:, 1, 0:1], in_=thr)
-        gate_list = sb.tile([P, I // 16], U16)
+        row_terms_loaded = sb.tile([P, 2, DMA_BLOCK], F32)
+        nc.gpsimd.dma_start(out=row_terms_loaded[:, 0, 0:1], in_=slope)
+        nc.sync.dma_start(out=row_terms_loaded[:, 1, 0:1], in_=thr)
+        gate_list = sb.tile([P, I // HEAD_ROWS], U16)
         nc.sync.dma_start(gate_list[:], offs2)
-        note_words = sb.tile([P, 2 * U], U8, align_bytes=64)
+        note_words = sb.tile([P, 2 * U], U8, align_bytes=MX_ALIGN)
         nc.sync.dma_start(out=note_words[:].bitcast(I32), in_=notes_words[0].bitcast(I32))
-        note_plane = sb.tile([P, U], U8, align_bytes=64)
-        load_scale_rows(nc.sync, note_plane, notes_scales)
-        out_list = sb.tile([P, I // 16], U16)
+        note_plane = sb.tile([P, U], U8, align_bytes=MX_ALIGN)
+        load_scale_rows((nc.sync,) * (P // QUADRANT), note_plane, notes_scales)
+        out_list = sb.tile([P, I // HEAD_ROWS], U16)
         nc.sync.dma_start(out_list[:], offs3)
 
-        q_grouped = sb.tile([P, Q, PACK], BF16, align_bytes=64)
-        q_words = sb.tile([P, Q], U32, align_bytes=64)
-        q_plane = sb.tile([P, Q], U8, align_bytes=64)
-        halves = [slice(h * Q // 2, (h + 1) * Q // 2) for h in range(2)]
-        for rows in halves:
+        q_grouped = sb.tile([P, Q, PACK], BF16, align_bytes=MX_ALIGN)
+        q_words = sb.tile([P, Q], U32, align_bytes=MX_ALIGN)
+        q_plane = sb.tile([P, Q], U8, align_bytes=MX_ALIGN)
+        q_halves = (slice(0, Q // 2), slice(Q // 2, Q))
+        for rows in q_halves:
             nc.vector.tensor_copy(
-                out=q_grouped[:, rows, :].rearrange("p (c i) j -> p c j i", i=4),
-                in_=q_raw[:, :, rows].rearrange("p j (c i) -> p c j i", i=4),
+                out=q_grouped[:, rows, :].rearrange("p (c e) r -> p c r e", e=LINE),
+                in_=q_raw[:, :, rows].rearrange("p r (c e) -> p c r e", e=LINE),
             )
-        for rows in halves:
+        for rows in q_halves:
             nc.vector.quantize_mx(
-                out=q_words[:, rows].bitcast(FP8X4), scales=q_plane[:, rows],
-                in_=q_grouped[:, rows, :].rearrange("p q j -> p (q j)"),
+                out=q_words[:, rows].bitcast(FP8X4),
+                scales=q_plane[:, rows],
+                in_=q_grouped[:, rows, :].rearrange("p q r -> p (q r)"),
             )
 
         token_scores = sb.tile([P, T], F32)
-        for start in range(0, T, TOKEN_PASS):
-            cols = slice(start, start + TOKEN_PASS)
-            h, lo = divmod(start, BANK)
-            acc = ps.tile([P, BANK], F32, name="token_acc%d" % start)[:, :TOKEN_PASS]
+        for first in range(0, T, TOKEN_PASS):
+            cols = slice(first, first + TOKEN_PASS)
+            half, within = divmod(first, BANK)
+            token_acc = ps.tile([P, BANK], F32, name="token_acc%d" % first)[:, :TOKEN_PASS]
             nc.tensor.matmul_mx(
-                out=acc, lhsT=q_words[:].bitcast(FP8X4), lhsT_scale=q_plane[:],
-                rhs=key_words[h][:, lo : lo + TOKEN_PASS].bitcast(FP8X4), rhs_scale=key_plane[:, cols],
-                start=True, stop=True,
+                out=token_acc,
+                lhsT=q_words[:].bitcast(FP8X4),
+                lhsT_scale=q_plane[:],
+                rhs=key_words[half][:, within : within + TOKEN_PASS].bitcast(FP8X4),
+                rhs_scale=key_plane[:, cols],
+                start=True,
+                stop=True,
             )
-            nc.vector.tensor_copy(out=token_scores[:, cols], in_=acc)
+            nc.vector.tensor_copy(out=token_scores[:, cols], in_=token_acc)
 
-        gate_terms = sb.tile([P, 2], F32)
-        nc.vector.tensor_copy(out=gate_terms[:], in_=gate_loaded[:, :, 0])
+        row_terms = sb.tile([P, 2], F32)
+        nc.vector.tensor_copy(out=row_terms[:], in_=row_terms_loaded[:, :, 0])
 
         note_acc = []
-        for h in range(U // BANK):
-            acc = ps.tile([P, BANK], F32, name="note_acc%d" % h)
+        for half in range(U // BANK):
+            bank = ps.tile([P, BANK], F32, name="note_acc%d" % half)
             nc.tensor.matmul_mx(
-                out=acc[:], lhsT=q_words[:].bitcast(FP8X4), lhsT_scale=q_plane[:],
-                rhs=note_words[:, 2 * h * BANK : 2 * (h + 1) * BANK].bitcast(FP4X4),
-                rhs_scale=note_plane[:, h * BANK : (h + 1) * BANK], start=True, stop=True,
+                out=bank[:],
+                lhsT=q_words[:].bitcast(FP8X4),
+                lhsT_scale=q_plane[:],
+                rhs=note_words[:, 2 * half * BANK : 2 * (half + 1) * BANK].bitcast(FP4X4),
+                rhs_scale=note_plane[:, half * BANK : (half + 1) * BANK],
+                start=True,
+                stop=True,
             )
-            note_acc.append(acc)
+            note_acc.append(bank)
 
-        for s in range(I // PIECE):
-            entries = slice(s * LIST_COLS, (s + 1) * LIST_COLS)
-            opened = sb.tile([P, PIECE], F32, name="opened%d" % s)
+        for piece in range(I // PIECE):
+            opened = sb.tile([P, PIECE], F32, name="opened%d" % piece)
             nc.scalar.activation(
-                opened[:], token_scores[:].indirect(token_list[:, entries]), ACT.Sigmoid,
-                bias=gate_terms[:, 1:2], scale=gate_terms[:, 0:1],
+                opened[:],
+                token_scores[:].indirect(list_piece(token_list, piece)),
+                ACT.Sigmoid,
+                bias=row_terms[:, 1:2],
+                scale=row_terms[:, 0:1],
             )
-            nc.vector.tensor_copy(gates[:].indirect(gate_list[:, entries]), opened[:])
+            nc.vector.tensor_tensor(gates[:].indirect(list_piece(gate_list, piece)), opened[:], opened[:], ALU.add)
 
         sums = sb.tile([P, U], F32)
-        for h in range(U // BANK):
-            cols = slice(h * BANK, (h + 1) * BANK)
-            nc.vector.scalar_tensor_tensor(
-                out=sums[:, cols], in0=gates[:, cols], scalar=2.0, in1=note_acc[h][:], op0=ALU.mult, op1=ALU.add
-            )
+        note_tail = sb.tile([P, U - SPLIT], F32)
+        nc.scalar.copy(out=note_tail[:], in_=note_acc[1][:, SPLIT - BANK :])
+        nc.gpsimd.tensor_tensor(sums[:, SPLIT:], gates[:, SPLIT:], note_tail[:], ALU.add)
+        nc.vector.tensor_tensor(sums[:, :BANK], gates[:, :BANK], note_acc[0][:], ALU.add)
+        nc.vector.tensor_tensor(sums[:, BANK:SPLIT], gates[:, BANK:SPLIT], note_acc[1][:, : SPLIT - BANK], ALU.add)
         neg_top = sb.tile([P, 1], F32)
         nc.vector.tensor_reduce(out=neg_top[:], in_=sums[:], axis=mybir.AxisListType.X, op=ALU.max, negate=True)
 
-        for s in range(I // PIECE):
-            entries = slice(s * LIST_COLS, (s + 1) * LIST_COLS)
-            result = sb.tile([P, PIECE], F32, name="result%d" % s)
-            nc.scalar.activation(result[:], sums[:].indirect(out_list[:, entries]), ACT.Exp, bias=neg_top[:])
-            nc.sync.dma_start(out=out[:, s * PIECE : (s + 1) * PIECE], in_=result[:])
+        for piece in range(I // PIECE):
+            result = sb.tile([P, PIECE], F32, name="result%d" % piece)
+            nc.scalar.activation(result[:], sums[:].indirect(list_piece(out_list, piece)), ACT.Exp, bias=neg_top[:])
+            nc.sync.dma_start(out=out[:, piece * PIECE : (piece + 1) * PIECE], in_=result[:])

from contextlib import ExitStack

import concourse.mybir as mybir

D, T, U, I, Q = 512, 1024, 1024, 512, 128
FLOPS = 2 * D * Q * (T + U)

F32 = mybir.dt.float32
BF16 = mybir.dt.bfloat16
I32 = mybir.dt.int32
U32 = mybir.dt.uint32
U16 = mybir.dt.uint16
U8 = mybir.dt.uint8
FP8X4 = mybir.dt.float8_e4m3fn_x4
FP4X4 = mybir.dt.float4_e2m1fn_x4
ALU = mybir.AluOpType
ACT = mybir.ActivationFunctionType

P = 128
PACK = 4
QUADRANT = 32
SCALE_ROWS = 4
HEAD_ROWS = 16
MX_ALIGN = 64
BANK = 512
LINE = 4
DMA_BLOCK = 8
TOKEN_PASS = 256
PIECE = 256
SPLIT = 704


def load_scale_rows(queues, plane, scales):
    for quad, queue in enumerate(queues):
        queue.dma_start(
            out=plane[QUADRANT * quad : QUADRANT * quad + SCALE_ROWS, :].bitcast(I32),
            in_=scales[0, SCALE_ROWS * quad : SCALE_ROWS * (quad + 1), :].bitcast(I32),
        )


def list_piece(list_tile, piece):
    width = PIECE // HEAD_ROWS
    return list_tile[:, piece * width : (piece + 1) * width]


def tile_attend_openedfirst_two_kernel(
    tc, query, keys_words, keys_scales, notes_words, notes_scales, thr, slope, offs, offs2, offs3, out
):
    nc = tc.nc
    with ExitStack() as ctx:
        sb = ctx.enter_context(tc.tile_pool(name="sb", bufs=1))
        ps = ctx.enter_context(tc.psum_pool(name="ps", bufs=1))

        gates = sb.tile([P, U], F32)
        nc.vector.memset(gates[:], 0.0)

        q_raw = sb.tile([P, PACK, Q], F32)
        nc.sync.dma_start(out=q_raw[:], in_=query.rearrange("(p r) q -> p r q", r=PACK))
        key_plane = sb.tile([P, T], U8, align_bytes=MX_ALIGN)
        load_scale_rows((nc.sync, nc.sync, nc.scalar, nc.scalar), key_plane, keys_scales)
        token_list = sb.tile([P, I // HEAD_ROWS], U16)
        nc.sync.dma_start(token_list[:], offs)
        key_src = keys_words[0].rearrange("p t r -> p (t r)").bitcast(I32)
        key_words = []
        for half in range(T // BANK):
            words = sb.tile([P, BANK], U32, align_bytes=MX_ALIGN, name="key_words%d" % half)
            nc.sync.dma_start(out=words[:].bitcast(I32), in_=key_src[:, half * BANK : (half + 1) * BANK])
            key_words.append(words)
        row_terms_loaded = sb.tile([P, 2, DMA_BLOCK], F32)
        nc.gpsimd.dma_start(out=row_terms_loaded[:, 0, 0:1], in_=slope)
        nc.sync.dma_start(out=row_terms_loaded[:, 1, 0:1], in_=thr)
        gate_list = sb.tile([P, I // HEAD_ROWS], U16)
        nc.sync.dma_start(gate_list[:], offs2)
        note_words = sb.tile([P, 2 * U], U8, align_bytes=MX_ALIGN)
        nc.sync.dma_start(out=note_words[:].bitcast(I32), in_=notes_words[0].bitcast(I32))
        note_plane = sb.tile([P, U], U8, align_bytes=MX_ALIGN)
        load_scale_rows((nc.sync,) * (P // QUADRANT), note_plane, notes_scales)
        out_list = sb.tile([P, I // HEAD_ROWS], U16)
        nc.sync.dma_start(out_list[:], offs3)

        q_grouped = sb.tile([P, Q, PACK], BF16, align_bytes=MX_ALIGN)
        q_words = sb.tile([P, Q], U32, align_bytes=MX_ALIGN)
        q_plane = sb.tile([P, Q], U8, align_bytes=MX_ALIGN)
        q_halves = (slice(0, Q // 2), slice(Q // 2, Q))
        for rows in q_halves:
            nc.vector.tensor_copy(
                out=q_grouped[:, rows, :].rearrange("p (c e) r -> p c r e", e=LINE),
                in_=q_raw[:, :, rows].rearrange("p r (c e) -> p c r e", e=LINE),
            )
        for rows in q_halves:
            nc.vector.quantize_mx(
                out=q_words[:, rows].bitcast(FP8X4),
                scales=q_plane[:, rows],
                in_=q_grouped[:, rows, :].rearrange("p q r -> p (q r)"),
            )

        token_scores = sb.tile([P, T], F32)
        for first in range(0, T, TOKEN_PASS):
            cols = slice(first, first + TOKEN_PASS)
            half, within = divmod(first, BANK)
            token_acc = ps.tile([P, BANK], F32, name="token_acc%d" % first)[:, :TOKEN_PASS]
            nc.tensor.matmul_mx(
                out=token_acc,
                lhsT=q_words[:].bitcast(FP8X4),
                lhsT_scale=q_plane[:],
                rhs=key_words[half][:, within : within + TOKEN_PASS].bitcast(FP8X4),
                rhs_scale=key_plane[:, cols],
                start=True,
                stop=True,
            )
            nc.vector.tensor_copy(out=token_scores[:, cols], in_=token_acc)

        row_terms = sb.tile([P, 2], F32)
        nc.vector.tensor_copy(out=row_terms[:], in_=row_terms_loaded[:, :, 0])

        note_acc = []
        for half in range(U // BANK):
            bank = ps.tile([P, BANK], F32, name="note_acc%d" % half)
            nc.tensor.matmul_mx(
                out=bank[:],
                lhsT=q_words[:].bitcast(FP8X4),
                lhsT_scale=q_plane[:],
                rhs=note_words[:, 2 * half * BANK : 2 * (half + 1) * BANK].bitcast(FP4X4),
                rhs_scale=note_plane[:, half * BANK : (half + 1) * BANK],
                start=True,
                stop=True,
            )
            note_acc.append(bank)

        for piece in range(I // PIECE):
            opened = sb.tile([P, PIECE], F32, name="opened%d" % piece)
            nc.scalar.activation(
                opened[:],
                token_scores[:].indirect(list_piece(token_list, piece)),
                ACT.Sigmoid,
                bias=row_terms[:, 1:2],
                scale=row_terms[:, 0:1],
            )
            nc.vector.tensor_tensor(gates[:].indirect(list_piece(gate_list, piece)), opened[:], opened[:], ALU.add)

        sums = sb.tile([P, U], F32)
        note_tail = sb.tile([P, U - SPLIT], F32)
        nc.scalar.copy(out=note_tail[:], in_=note_acc[1][:, SPLIT - BANK :])
        nc.gpsimd.tensor_tensor(sums[:, SPLIT:], gates[:, SPLIT:], note_tail[:], ALU.add)
        nc.vector.tensor_tensor(sums[:, :BANK], gates[:, :BANK], note_acc[0][:], ALU.add)
        nc.vector.tensor_tensor(sums[:, BANK:SPLIT], gates[:, BANK:SPLIT], note_acc[1][:, : SPLIT - BANK], ALU.add)
        neg_top = sb.tile([P, 1], F32)
        nc.vector.tensor_reduce(out=neg_top[:], in_=sums[:], axis=mybir.AxisListType.X, op=ALU.max, negate=True)

        for piece in range(I // PIECE):
            result = sb.tile([P, PIECE], F32, name="result%d" % piece)
            nc.scalar.activation(result[:], sums[:].indirect(list_piece(out_list, piece)), ACT.Exp, bias=neg_top[:])
            nc.sync.dma_start(out=out[:, piece * PIECE : (piece + 1) * PIECE], in_=result[:])
